import numpy as np, ml_dtypes
CORES = [2,3,42,43,82,83,122,123]
N = 8
import mx_ref
BF = ml_dtypes.bfloat16
def cols(t, e):
    v = np.concatenate([t.reshape(128, -1, 4), np.zeros((128, 1, 4), BF)], axis=1)
    return np.ascontiguousarray(v[:, e]).reshape(128, -1)
def cut(t, i, w=512):
    return t[:, w * i:w * i + w]
def f(rng, *shape):
    return mx_ref.flush((rng.standard_normal(shape, dtype=np.float32) * np.exp2(rng.integers(-2, 3, shape[:-1] + (1,)))).astype(BF))
def wide(rng, *shape, cols=0):
    v = rng.standard_normal(shape, dtype=np.float32) * np.exp2(rng.integers(-12, 13, shape)).astype(np.float32)
    if cols: v *= np.repeat(np.exp2(rng.integers(-cols, cols + 1, shape[:-2] + (1, shape[-1] // 4))) * (rng.random(shape[:-2] + (1, shape[-1] // 4)) > 0.0625), 4, axis=-1).astype(np.float32)
    return mx_ref.flush(v.astype(BF))
P, K, R, O = 512, 16, 4, 1
def bf(v):
    return mx_ref.flush(np.asarray(v, np.float32).astype(BF))
def same(v):
    t = np.zeros((128, 512), BF)
    t[:, :4] = v
    return np.stack([t] * N)
def setup_inputs(rng):
    return {"x": f(rng, N, 128, 4 * P), "u": same(f(rng, 128, 4)), "w": f(rng, N, 128, 512 * O)}
def setup_inputs_ties(rng):
    d = setup_inputs(rng)
    T = (P - K - 1) // 3
    H = T // 2
    shared = f(rng, 128, 4 * H)
    x = []
    for r in range(N):
        pool = np.concatenate([shared, f(rng, 128, 4 * (T + 1 - H))], axis=1)
        e = np.concatenate([np.repeat(np.arange(T), 3), np.full(P - 3 * T, T)])
        x.append(cols(pool, rng.permutation(e)))
    d["x"] = np.stack(x)
    d["u"] = bf(d["u"].astype(np.float32) * np.float32(256))
    return d
def setup_inputs_like(rng):
    d = setup_inputs(rng)
    at = rng.permutation(8)
    size = np.zeros(8)
    size[at] = np.exp2(-3.0 - np.arange(8) // 2)
    d["u"] = same(bf((1 + 0.25 * rng.random((128, 4))) * np.repeat(size, 16)[:, None]))
    side = rng.permutation(N) % 2
    x = []
    for r in range(N):
        c = rng.permutation(np.arange(P) % 8)
        h = np.where(c % 2 == side[r], 1.0, 0.75)
        on = np.repeat(np.arange(8)[:, None] == at[c][None, :], 16, axis=0) * h[None, :]
        x.append(bf((on[:, :, None] * (1 + 0.25 * rng.random((128, P, 4))) + 2.0 ** -8 * rng.standard_normal((128, P, 4))).reshape(128, 4 * P)))
    d["x"] = np.stack(x)
    return d
def setup_inputs_late(rng):
    d = setup_inputs(rng)
    half = (np.arange(128) < 64) ^ bool(rng.integers(0, 2))
    d["u"] = same(bf(2.0 ** 28 * (R - 1.5) * (1 + 0.25 * rng.random((128, 4))) * half[:, None]))
    x = []
    for r in range(N):
        late = rng.permutation(P) < rng.integers(2 * K, P // 2 + 1)
        v = np.where(half, 2.0 ** 22, 2.0 ** 26)[:, None] * np.where(late, -1.0, 1.0)[None, :]
        x.append(bf((v[:, :, None] * (1 + 0.25 * rng.random((128, P, 4)))).reshape(128, 4 * P)))
    d["x"] = np.stack(x)
    return d
def setup_inputs_low(rng):
    d = setup_inputs(rng)
    size = np.full((N, P), 2.0 ** 29)
    for r in range(N):
        e = 32 * int(rng.integers(0, P // 32)) + rng.permutation(32)[:K]
        size[r, e] = 2.0 ** 28
        size[r, e[:int(rng.integers(2, K // 2 + 1))]] = 0
    d["x"] = bf(np.repeat(size, 4, axis=1)[:, None, :] * (1.5 + 0.45 * rng.random((N, 128, 4 * P))))
    d["u"] = same(bf(-2.0 ** 29 * (1.5 + 0.45 * rng.random((128, 4)))))
    return d
def setup_inputs_spread(rng):
    d = setup_inputs(rng)
    d["x"] = wide(rng, N, 128, 4 * P, cols=6)
    d["u"] = same(bf(wide(rng, 128, 4).astype(np.float32) * np.float32(256)))
    return d
def check_inputs(d):
    b = []
    for k in ("x", "u", "w"):
        v = np.abs(d[k].astype(np.float32))
        if not (np.isfinite(v).all() and ((v == 0) | (v >= 2.0 ** -30) & (v <= 2.0 ** 30)).all()): b.append("a value of " + k)
    v = d["u"].astype(np.float32)
    if (v[:, :, 4:] != 0).any(): b.append("u has numbers behind its first column")
    if (v != v[:1]).any(): b.append("u isn't the same on all ranks")
    return b
def reference(x, u, w):
    X = [mx_ref.quantize(np.ascontiguousarray(x[r])) for r in range(N)]
    s = [mx_ref.matmul(mx_ref.quantize(np.ascontiguousarray(u[r])), X[r])[0] + np.float32(0.0) for r in range(N)]
    free = np.ones((N, P), bool)
    ch, se, y = np.zeros((N, R, K), np.float32), np.zeros((N, 1, P), np.float32), np.zeros((N, 128, O * R * 128), np.float32)
    M = []
    for b in range(R):
        best = []
        for r in range(N):
            e = np.argsort(np.where(free[r], -s[r], np.float32(np.inf)), kind="stable")[:K]
            free[r, e] = False
            ch[r, b] = e
            best.append(cols(x[r], e))
        M.append(mx_ref.quantize(np.ascontiguousarray(np.concatenate(best, axis=1))))
        if b < R - 1:
            for r in range(N):
                m = mx_ref.matmul(M[b], X[r]).max(axis=0) + np.float32(0.0)
                s[r] = s[r] - np.float32(0.25) * m
    for r in range(N):
        se[r, 0] = s[r]
        for o in range(O):
            q = mx_ref.quantize(np.ascontiguousarray(cut(w[r], o)))
            for b in range(R):
                i = (o * R + b) * 128
                y[r, :, i:i + 128] = mx_ref.matmul(q, M[b])
    return {"ch": ch, "se": se, "y": y}

@@ -1,0 +1,355 @@
+from concourse.bass import DstId, RemoteDMATransfer
+from concourse.mybir import dt, AluOpType, AxisListType, ActivationFunctionType
+
+R = 4
+COPY = ActivationFunctionType.Copy
+IDENT = ActivationFunctionType.Identity
+A = AluOpType
+BIG = 1e29
+
+SCRATCH = {
+    "xt": ("sbuf", [128, 2048], "bfloat16"),
+    "ut": ("sbuf", [128, 512], "bfloat16"),
+    "wt": ("sbuf", [128, 512], "bfloat16"),
+    "xq": ("sbuf", [128, 512], "float8_e4m3fn_x4"),
+    "xs": ("sbuf", [128, 512], "uint8"),
+    "pq": ("sbuf", [128, 512], "float8_e4m3fn_x4"),
+    "pz": ("sbuf", [128, 512], "uint8"),
+    "uq": ("sbuf", [128, 128], "float8_e4m3fn_x4"),
+    "us": ("sbuf", [128, 128], "uint8"),
+    "vq": ("sbuf", [128, 128], "float8_e4m3fn_x4"),
+    "vs": ("sbuf", [128, 128], "uint8"),
+    "wq": ("sbuf", [128, 128], "float8_e4m3fn_x4"),
+    "ws": ("sbuf", [128, 128], "uint8"),
+    "ip": ("sbuf", [128, 1], "int32"),
+    "ir": ("sbuf", [128, 2], "int32"),
+    "rc": ("sbuf", [128, 4], "float32"),
+    "ki": ("sbuf", [128, 32], "float32"),
+    "k16": ("sbuf", [128, 32], "float32"),
+    "kim": ("sbuf", [128, 32], "float32"),
+    "mbig": ("sbuf", [128, 32], "float32"),
+    "rb": ("sbuf", [128, 32], "float32"),
+    "j4": ("sbuf", [128, 4], "float32"),
+    "jc": ("sbuf", [128, 4], "float32"),
+    "pm": ("sbuf", [128, 32], "float32"),
+    "po": ("sbuf", [128, 32], "uint16"),
+    "zo": ("sbuf", [128, 8], "uint16"),
+    "nq": ("sbuf", [128, 32], "float32"),
+    "z32": ("sbuf", [128, 32], "float32"),
+    "B": ("sbuf", [128, 128 * R], "float32"),
+    "Q": ("sbuf", [128, 128 * R], "float32"),
+    "bm": ("sbuf", [128, 128 * R], "float32"),
+    "cmp": ("sbuf", [128, 640 * R], "bfloat16"),
+    "junk": ("sbuf", [128, 640 * R], "bfloat16"),
+    "jj": ("sbuf", [128, 128 * R], "float32"),
+    "lr": ("sbuf", [128, 4 * R], "float32"),
+    "wv": ("sbuf", [128, 128 * R], "float32"),
+    "wj": ("sbuf", [128, 128 * R], "float32"),
+    "wvt": ("sbuf", [128, 128 * R], "float32"),
+    "wjt": ("sbuf", [128, 128 * R], "float32"),
+    "vc": ("sbuf", [128, R], "float32"),
+    "jcol": ("sbuf", [128, R], "float32"),
+    "bv": ("sbuf", [128, 32 * R], "float32"),
+    "vt": ("sbuf", [128, 32 * R], "float32"),
+    "gg": ("sbuf", [128, 96 * R], "float32"),
+    "c2": ("sbuf", [128, 96 * R], "float32"),
+    "n2": ("sbuf", [128, R], "float32"),
+    "w2": ("sbuf", [128, 32 * R], "float32"),
+    "w2x": ("sbuf", [128, 80 * R], "float32"),
+    "lf": ("sbuf", [128, R], "float32"),
+    "lb": ("sbuf", [128, 32 * R], "float32"),
+    "lt": ("sbuf", [128, 32 * R], "float32"),
+    "ind": ("sbuf", [128, 32 * R], "float32"),
+    "indt": ("sbuf", [128, 32 * R], "float32"),
+    "tt": ("sbuf", [128, R], "float32"),
+    "pen": ("sbuf", [128, 4 * R], "float32"),
+    "sm": ("sbuf", [128, 4 * R], "float32"),
+    "mm": ("sbuf", [128, 4 * R], "float32"),
+    "m25": ("sbuf", [128, 4 * R], "float32"),
+    "sc": ("sbuf", [128, 4 * R], "float32"),
+    "sb": ("sbuf", [128, 128], "float32"),
+    "sr": ("sbuf", [128, 128], "float32"),
+    "yo": ("sbuf", [128, 512], "float32"),
+    "ps": ("psum", [128, 2048], "float32"),
+    "py": ("psum", [128, 2048], "float32"),
+}
+for _b in range(R):
+    SCRATCH["of%d" % _b] = ("sbuf", [128, 2], "uint16")
+    SCRATCH["mq%d" % _b] = ("sbuf", [128, 128], "float8_e4m3fn_x4")
+    SCRATCH["ms%d" % _b] = ("sbuf", [128, 128], "uint8")
+
+SEMAPHORES = ["sv", "sa", "st", "sg", "du", "dw", "dse", "loc"]
+SEMAPHORES += ["dx%d" % i for i in range(4)]
+SEMAPHORES += ["%s%d" % (n, b) for n in ("near", "far", "dy", "dch") for b in range(R)]
+
+
+def mask_of(engines):
+    return sum(1 << e for e in engines)
+
+
+def rank_program(g, core, T, topo):
+    rank = T.rank_of(core)
+    if rank is None:
+        return
+    cores = list(T.cores)
+    here = topo.chip(core)
+    mate_rank = [r for r in range(len(cores)) if r != rank and topo.chip(cores[r]) == here][0]
+    lo = min(rank, mate_rank)
+    peers = [r for r in range(len(cores)) if topo.chip(cores[r]) != here and r % 2 == rank % 2]
+    far_eng = topo.engines(core, cores[peers[0]])
+    near_eng = topo.engines(core, cores[mate_rank])[:len(far_eng)]
+
+    Q = {"v": g.vector, "a": g.scalar, "t": g.tensor, "g": g, "s": g.sync}
+    count = {"v": 0, "a": 0, "t": 0, "g": 0}
+    seen = {k: {} for k in Q}
+
+    def wait(q, deps):
+        need = {}
+        for d in deps:
+            for s, n in (d if isinstance(d, list) else [d]):
+                need[s] = max(need.get(s, 0), n)
+        for s, n in need.items():
+            if seen[q].get(s, 0) < n:
+                Q[q].wait_ge(T.sem[s], n)
+                seen[q][s] = n
+
+    def done(q, ins):
+        count[q] += 1
+        ins.then_inc(T.sem["s" + q], 1)
+        return ("s" + q, count[q])
+
+    def ts(out, in0, s1, op0, *deps, s2=None, op1=None):
+        wait("v", deps)
+        if op1 is None:
+            return done("v", g.vector.tensor_scalar(out, in0, s1, None, op0))
+        return done("v", g.vector.tensor_scalar(out, in0, s1, s2, op0, op1))
+
+    def tt(out, a, b, op, *deps):
+        wait("v", deps)
+        return done("v", g.vector.tensor_tensor(out, a, b, op))
+
+    def red(out, in_, op, *deps):
+        wait("v", deps)
+        return done("v", g.vector.tensor_reduce(out, in_, AxisListType.X, op))
+
+    def turn(out, in_, *deps):
+        wait("v", deps)
+        return done("v", g.vector.transpose(out, in_))
+
+    def vcopy(out, in_, *deps):
+        wait("v", deps)
+        return done("v", g.vector.tensor_copy(out, in_))
+
+    def fill(out, c):
+        return done("v", g.vector.memset(out, c))
+
+    def quant(q, s, x, *deps):
+        wait("v", deps)
+        return done("v", g.vector.quantize_mx(q, s, x))
+
+    def act(out, in_, func, *deps, **kw):
+        wait("a", deps)
+        return done("a", g.scalar.activation(out, in_, func, **kw))
+
+    def mm(out, lq, ls, rq, rs, *deps):
+        wait("t", deps)
+        return done("t", g.tensor.matmul_mx(out, lq, ls, rq, rs, True, True))
+
+    def load(q, out, in_, sem, *deps, n=1):
+        wait(q, deps)
+        Q[q].dma_start(out, in_).then_inc(T.sem[sem], 16)
+        return (sem, 16 * n)
+
+    lu = load("a", T.ut[:], T.u[:], "du")
+    lx = [load("s" if i % 2 == 0 else "a", T.xt[:, 512 * i:512 * i + 512], T.x[:, 512 * i:512 * i + 512], "dx%d" % i)
+          for i in range(4)]
+    lw = load("s", T.wt[:], T.w[:], "dw")
+
+    iota = lambda out, pat, cm, **kw: done("g", g.iota(out, pat, 0, cm, **kw))
+    flag = {"allow_small_or_imprecise_dtypes": True}
+    k_zo = fill(T.zo[:], 0)
+    k_ip = iota(T.ip[:], [[0, 1]], 1)
+    k_ki = iota(T.ki[:], [[1, 32]], 0, **flag)
+    k_16 = iota(T.k16[:], [[0, 2], [1, 16]], 0, **flag)
+    k_j4 = iota(T.j4[:], [[32, 4]], 4, **flag)
+    k_pm = iota(T.pm[:], [[32, 4], [128, 4], [16, 2]], 0, **flag)
+    fill(T.nq[:], -0.25)
+    k_z = fill(T.z32[:], 0.0)
+    k_gg = fill(T.gg[:], -BIG)
+    a1 = ts(T.ir[:, 0:1], T.ip[:], 31, A.bitwise_and, k_ip)
+    a2 = ts(T.ir[:, 1:2], T.ip[:], 15, A.bitwise_and)
+    k_rc = vcopy(T.rc[:, 0:2], T.ir[:], a1, a2)
+    k_r3 = ts(T.rc[:, 2:3], T.rc[:, 0:1], 3.0, A.mult, k_rc)
+    ts(T.kim[:], T.k16[:], T.rc[:, 0:1], A.subtract, k_16)
+    k_mb = ts(T.mbig[:], T.ki[:], T.rc[:, 0:1], A.is_ge, k_ki, s2=BIG, op1=A.mult)
+    ts(T.rb[:], T.z32[:], T.rc[:, 0:1], A.add, k_z)
+    k_po = ts(T.po[:], T.pm[:], T.rc[:, 1:2], A.add, k_pm)
+    k_con = ts(T.jc[:], T.j4[:], T.rc[:, 2:3], A.subtract, k_j4, k_r3)
+
+    qu = quant(T.uq[:], T.us[:], T.ut[:], lu)
+    u1 = vcopy(T.vq[:].bitcast(dt.uint32), T.uq[:].bitcast(dt.uint32).indirect(T.zo[:, 0:8]), qu, k_zo)
+    u2 = act(T.vs[:], T.us[:].indirect(T.zo[:, 0:8]), COPY, qu, k_zo)
+    tq, qx = [], []
+    for i in range(4):
+        c = slice(128 * i, 128 * i + 128)
+        qx.append(quant(T.xq[:, c], T.xs[:, c], T.xt[:, 512 * i:512 * i + 512], lx[i]))
+    for i in range(4):
+        c = slice(128 * i, 128 * i + 128)
+        h = slice(32 * i, 32 * i + 32)
+        t = mm(T.ps[:, 512 * i:512 * i + 128], T.vq[:], T.vs[:], T.xq[:, c], T.xs[:, c], u1, u2, qx[i])
+        if i % 2 == 0:
+            tq.append(vcopy(T.Q[h, 0:128], T.ps[h, 512 * i:512 * i + 128], t))
+        else:
+            tq.append(act(T.Q[h, 0:128], T.ps[h, 512 * i:512 * i + 128], COPY, t))
+    tb = [turn(T.B[:, 0:128], T.Q[:, 0:128], *tq, k_con)] * 4
+    bank_free = list(tq)
+    y_todo = []
+    qw = perm = None
+    t_m = [None] * 4
+
+    def span(a, n):
+        return slice(32 * a, 32 * a + 32 * n)
+    moves = [(span(0, 2), span(2, 2), 0, 1), (span(2, 2), span(0, 2), 0, 0)]
+    for x, slot in ((1, 1), (3, 2)):
+        for a in range(4):
+            moves.append((span(a, 1), span(a ^ x, 1), slot, 1 if (a ^ x) > a else 0))
+
+    for b in range(R):
+        o = 128 * b
+        if b > 0:
+            tq = [turn(T.Q[:, o:o + 128], T.B[:, o:o + 128], *tb)]
+        bm = [act(T.bm[:, o + 32 * c:o + 32 * c + 32], T.mbig[:], IDENT, tb[c], k_mb,
+                  bias=T.B[:, o + 32 * c:o + 32 * c + 1]) for c in range(4)]
+        lr = []
+        for c in range(4):
+            s = T.B[:, o + 32 * c:o + 32 * c + 1]
+            w = 640 * b + 160 * c
+            d = []
+            if c > 0:
+                d.append(ts(T.cmp[:, w:w + 32 * c], T.Q[:, o:o + 32 * c], s, A.is_ge, tq, tb))
+            d.append(ts(T.cmp[:, w + 32 * c:w + 128], T.Q[:, o + 32 * c:o + 128], s, A.is_gt, tq, tb))
+            d.append(tt(T.cmp[:, w + 128:w + 160], T.Q[:, o + 32 * c:o + 32 * c + 32],
+                        T.bm[:, o + 32 * c:o + 32 * c + 32], A.is_equal, bm[c]))
+            lr.append(act(T.junk[:, w:w + 160], T.cmp[:, w:w + 160], COPY, d, accum_out=T.lr[:, 4 * b + c:4 * b + c + 1]))
+
+        def onehot(dst, c, val):
+            return ts(dst[:, o + 32 * c:o + 32 * c + 32], T.ki[:], T.lr[:, 4 * b + c:4 * b + c + 1], A.is_equal, lr[c],
+                      s2=val, op1=A.mult)
+        wv = [onehot(T.wv, c, T.B[:, o + 32 * c:o + 32 * c + 1]) for c in range(4)]
+        wj = [onehot(T.wj, 0, T.jc[:, 0:1])]
+        t2 = turn(T.wvt[:, o:o + 128], T.wv[:, o:o + 128], wv)
+        wj += [onehot(T.wj, c, T.jc[:, c:c + 1]) for c in (1, 2)]
+        vc = red(T.vc[:, b:b + 1], T.wvt[:, o:o + 128], A.add, t2)
+        wj.append(onehot(T.wj, 3, T.jc[:, 3:4]))
+        v32 = slice(32 * b, 32 * b + 32)
+        bv = ts(T.bv[:, v32], T.z32[:], T.vc[:, b:b + 1], A.add, vc)
+        tj = turn(T.wjt[:, o:o + 128], T.wj[:, o:o + 128], wj)
+        t3 = turn(T.vt[:, v32], T.bv[:, v32], bv)
+
+        cp = []
+        for i, (to, fr, slot, half) in enumerate(moves):
+            at = 96 * b + 48 * half + 16 * slot
+            dst, src = T.gg[to, at:at + 16], T.vt[fr, 32 * b:32 * b + 16]
+            cp.append(vcopy(dst, src, t3, k_gg) if i % 2 == 0 else act(dst, src, COPY, t3, k_gg))
+        jcol = act(T.jj[:, o:o + 128], T.wjt[:, o:o + 128], COPY, tj, accum_out=T.jcol[:, b:b + 1])
+        g0 = 96 * b
+        f1 = ts(T.c2[:, g0:g0 + 48], T.gg[:, g0:g0 + 48], T.vc[:, b:b + 1], A.is_ge, cp)
+        f2 = ts(T.c2[:, g0 + 48:g0 + 96], T.gg[:, g0 + 48:g0 + 96], T.vc[:, b:b + 1], A.is_gt)
+        n2 = red(T.n2[:, b:b + 1], T.c2[:, g0:g0 + 96], A.add, f1, f2)
+        w2 = ts(T.w2[:, v32], T.kim[:], T.n2[:, b:b + 1], A.is_equal, n2, jcol, s2=T.jcol[:, b:b + 1], op1=A.mult)
+        x0 = 80 * b
+        t4 = turn(T.w2x[:, x0:x0 + 32], T.w2[:, v32], w2)
+        cp = []
+        for i, (to, fr, slot, half) in enumerate(moves):
+            at = x0 + 32 + 16 * slot
+            dst, src = T.w2x[to, at:at + 16], T.w2x[fr, x0:x0 + 16]
+            cp.append(vcopy(dst, src, t4) if i % 2 == 0 else act(dst, src, COPY, t4))
+        lf = red(T.lf[:, b:b + 1], T.w2x[:, x0:x0 + 80], A.add, cp, t4)
+        of = T["of%d" % b]
+        mq, ms = T["mq%d" % b], T["ms%d" % b]
+        oo = vcopy(of[:, 0:1], T.lf[:, b:b + 1], lf)
+        mine = slice(16 * rank, 16 * rank + 16)
+        both = slice(16 * lo, 16 * lo + 32)
+        pk = vcopy(mq[:, mine].bitcast(dt.uint32), T.xq[:].bitcast(dt.uint32).indirect(of[:, 0:1]), oo, qx)
+        pz = act(ms[:, mine], T.xs[:].indirect(of[:, 0:1]), COPY, oo, qx)
+
+        near, far = "near%d" % b, "far%d" % b
+        rid, pid = topo.addr(cores[mate_rank])[:2]
+        wait("g", [pk])
+        g.remote_dma(mq[:, mine].bitcast(dt.uint8), mq[:, mine].bitcast(dt.uint8), T.sem[near], T.sem.loc, pid, rid,
+                     mask_of(near_eng))
+        wait("g", [pz])
+        g.remote_dma(ms[:, mine], ms[:, mine], T.sem[near], T.sem.loc, pid, rid, mask_of(near_eng))
+        arr1 = (near, 2 * len(near_eng))
+        wait("g", [arr1])
+        ids = [DstId(rid=topo.addr(cores[r])[0], pnc=topo.addr(cores[r])[1]) for r in peers]
+        for view in (mq[:, both].bitcast(dt.uint8), ms[:, both]):
+            g.remote_dma_fused([RemoteDMATransfer(dst_ids=ids, dma_engine_mask=mask_of(far_eng), remote_sem=T.sem[far],
+                                                  srcs=[view], dsts=[view for r in peers])], local_sem=T.sem.loc)
+        arr2 = (far, 2 * len(far_eng) * len(peers))
+
+        if b == 0:
+            p1 = vcopy(T.pq[:].bitcast(dt.uint32), T.xq[:].bitcast(dt.uint32).indirect(T.po[:]), k_po)
+            p2 = act(T.pz[:], T.xs[:].indirect(T.po[:]), COPY, k_po, qx)
+            qw = quant(T.wq[:], T.ws[:], T.wt[:], lw)
+            perm = [p1, p2]
+            sc = None
+        if b < R - 1:
+            i1 = ts(T.ind[:, v32], T.rb[:], T.n2[:, b:b + 1], A.add, s2=16.0, op1=A.is_lt)
+            i2 = turn(T.indt[:, v32], T.ind[:, v32], i1)
+            i3 = red(T.tt[:, b:b + 1], T.indt[:, v32], A.add, i2)
+            b4 = slice(4 * b, 4 * b + 4)
+            i4 = ts(T.pen[:, b4], T.lr[:, b4], T.tt[:, b:b + 1], A.is_lt, i3, s2=-BIG, op1=A.mult)
+            sm = tt(T.sm[:, b4], T.B[:, o:o + 128:32], T.pen[:, b4], A.add, i4)
+        l1 = ts(T.lb[:, v32], T.z32[:], T.lf[:, b:b + 1], A.add)
+        l2 = turn(T.lt[:, v32], T.lb[:, v32], l1)
+        och = load("s", T.ch[b:b + 1, :], T.lt[0:1, 32 * b:32 * b + 16], "dch%d" % b, l2)
+        if b == 0:
+            sc = vcopy(T.sc[:, 0:4], T.B[:, 0:128:32])
+        else:
+            p4, b4 = slice(4 * b - 4, 4 * b), slice(4 * b, 4 * b + 4)
+            m1 = ts(T.m25[:, p4], T.mm[:, p4], -0.25, A.mult)
+            sc = tt(T.sc[:, b4], T.sc[:, p4], T.m25[:, p4], A.add, m1, sc)
+        if b == R - 1:
+            e = [ts(T.sb[:, 32 * c:32 * c + 32], T.z32[:], T.sc[:, 4 * b + c:4 * b + c + 1], A.add, sc) for c in range(4)]
+            e = turn(T.sr[:], T.sb[:], e)
+            for a in range(4):
+                load("s", T.se[0:1, 128 * a:128 * a + 128], T.sr[32 * a:32 * a + 1, :], "dse", e)
+        for f in y_todo:
+            f()
+        y_todo = []
+
+        ready = [arr1, arr2, pk, pz]
+        if b < R - 1:
+            tm = []
+            for c in range(4):
+                k = slice(128 * c, 128 * c + 128)
+                tm.append(mm(T.ps[:, 512 * c:512 * c + 128], T.pq[:, k], T.pz[:, k], mq[:], ms[:], *ready, *perm, *bank_free))
+            n = 128 * (b + 1)
+            rd, tb = [None] * 4, [None] * 4
+
+            def fall(c):
+                i = 4 * b + c
+                tb[c] = ts(T.B[:, n + 32 * c:n + 32 * c + 32], T.nq[:], T.mm[:, i:i + 1], A.mult, rd[c], sm,
+                           s2=T.sm[:, i:i + 1], op1=A.add)
+            for c in range(4):
+                rd[c] = red(T.mm[:, 4 * b + c:4 * b + c + 1], T.ps[:, 512 * c:512 * c + 128], A.max, tm[c])
+                if c > 0:
+                    fall(c - 1)
+            fall(3)
+            bank_free = list(rd)
+        ty = mm(T.py[:, 512 * b:512 * b + 128], T.wq[:], T.ws[:], mq[:], ms[:], *ready, qw)
+
+        def put(b=b, ty=ty):
+            k = slice(128 * b, 128 * b + 128)
+            t = act(T.yo[:, k], T.py[:, 512 * b:512 * b + 128], COPY, ty)
+            load("s", T.y[:, k], T.yo[:, k], "dy%d" % b, t)
+        y_todo.append(put)
+    for f in y_todo:
+        f()
+
+    sent = R * 2 * (len(near_eng) + len(far_eng))
+    last = [("loc", sent), ("dse", 64)] + [("s" + q, count[q]) for q in count]
+    last += [("dy%d" % b, 16) for b in range(R)] + [("dch%d" % b, 16) for b in range(R)]
+    last += [("far%d" % b, 2 * len(far_eng) * len(peers)) for b in range(R)]
+    wait("g", last)

@@ -4,83 +4,50 @@ from concourse.mybir import dt, AluOpType, AxisListType, ActivationFunctionType
 R = 4
 COPY = ActivationFunctionType.Copy
 IDENT = ActivationFunctionType.Identity
+ABS = ActivationFunctionType.Abs
+RELU = ActivationFunctionType.Relu
 A = AluOpType
 BIG = 1e29
 
+
+def sb(n, d="float32"):
+    return ("sbuf", [128, n], d)
+
+
+F8, U8, BF = "float8_e4m3fn_x4", "uint8", "bfloat16"
 SCRATCH = {
-    "xt": ("sbuf", [128, 2048], "bfloat16"),
-    "ut": ("sbuf", [128, 512], "bfloat16"),
-    "wt": ("sbuf", [128, 512], "bfloat16"),
-    "xq": ("sbuf", [128, 512], "float8_e4m3fn_x4"),
-    "xs": ("sbuf", [128, 512], "uint8"),
-    "pq": ("sbuf", [128, 512], "float8_e4m3fn_x4"),
-    "pz": ("sbuf", [128, 512], "uint8"),
-    "uq": ("sbuf", [128, 128], "float8_e4m3fn_x4"),
-    "us": ("sbuf", [128, 128], "uint8"),
-    "vq": ("sbuf", [128, 128], "float8_e4m3fn_x4"),
-    "vs": ("sbuf", [128, 128], "uint8"),
-    "wq": ("sbuf", [128, 128], "float8_e4m3fn_x4"),
-    "ws": ("sbuf", [128, 128], "uint8"),
-    "ip": ("sbuf", [128, 1], "int32"),
-    "ir": ("sbuf", [128, 2], "int32"),
-    "rc": ("sbuf", [128, 4], "float32"),
-    "ki": ("sbuf", [128, 32], "float32"),
-    "k16": ("sbuf", [128, 32], "float32"),
-    "kim": ("sbuf", [128, 32], "float32"),
-    "mbig": ("sbuf", [128, 32], "float32"),
-    "rb": ("sbuf", [128, 32], "float32"),
-    "j4": ("sbuf", [128, 4], "float32"),
-    "jc": ("sbuf", [128, 4], "float32"),
-    "pm": ("sbuf", [128, 32], "float32"),
-    "po": ("sbuf", [128, 32], "uint16"),
-    "zo": ("sbuf", [128, 8], "uint16"),
-    "nq": ("sbuf", [128, 32], "float32"),
-    "z32": ("sbuf", [128, 32], "float32"),
-    "B": ("sbuf", [128, 128 * R], "float32"),
-    "Q": ("sbuf", [128, 128 * R], "float32"),
-    "bm": ("sbuf", [128, 128 * R], "float32"),
-    "cmp": ("sbuf", [128, 640 * R], "bfloat16"),
-    "junk": ("sbuf", [128, 640 * R], "bfloat16"),
-    "jj": ("sbuf", [128, 128 * R], "float32"),
-    "lr": ("sbuf", [128, 4 * R], "float32"),
-    "wv": ("sbuf", [128, 128 * R], "float32"),
-    "wj": ("sbuf", [128, 128 * R], "float32"),
-    "wvt": ("sbuf", [128, 128 * R], "float32"),
-    "wjt": ("sbuf", [128, 128 * R], "float32"),
-    "vc": ("sbuf", [128, R], "float32"),
-    "jcol": ("sbuf", [128, R], "float32"),
-    "bv": ("sbuf", [128, 32 * R], "float32"),
-    "vt": ("sbuf", [128, 32 * R], "float32"),
-    "gg": ("sbuf", [128, 96 * R], "float32"),
-    "c2": ("sbuf", [128, 96 * R], "float32"),
-    "n2": ("sbuf", [128, R], "float32"),
-    "w2": ("sbuf", [128, 32 * R], "float32"),
-    "w2x": ("sbuf", [128, 80 * R], "float32"),
-    "lf": ("sbuf", [128, R], "float32"),
-    "lb": ("sbuf", [128, 32 * R], "float32"),
-    "lt": ("sbuf", [128, 32 * R], "float32"),
-    "ind": ("sbuf", [128, 32 * R], "float32"),
-    "indt": ("sbuf", [128, 32 * R], "float32"),
-    "tt": ("sbuf", [128, R], "float32"),
-    "pen": ("sbuf", [128, 4 * R], "float32"),
-    "sm": ("sbuf", [128, 4 * R], "float32"),
-    "mm": ("sbuf", [128, 4 * R], "float32"),
-    "m25": ("sbuf", [128, 4 * R], "float32"),
-    "sc": ("sbuf", [128, 4 * R], "float32"),
-    "sb": ("sbuf", [128, 128], "float32"),
-    "sr": ("sbuf", [128, 128], "float32"),
-    "yo": ("sbuf", [128, 512], "float32"),
-    "ps": ("psum", [128, 2048], "float32"),
-    "py": ("psum", [128, 2048], "float32"),
+    "xt": sb(2048, BF), "ut": sb(512, BF), "wt": sb(512, BF),
+    "xq": sb(512, F8), "xs": sb(512, U8),
+    "pq": sb(512, F8), "pz": sb(512, U8),
+    "uq": sb(128, F8), "us": sb(128, U8), "vq": sb(128, F8), "vs": sb(128, U8), "wq": sb(128, F8), "ws": sb(128, U8),
+    "ip": sb(1, "int32"), "ir": sb(2, "int32"),
+    "rc": sb(4),
+    "ki": sb(32),
+    "k16": sb(32),
+    "kim": sb(32),
+    "mbig": sb(32),
+    "rb": sb(32),
+    "c4": sb(4), "jn": sb(4), "nj": sb(4),
+    "pm": sb(32), "po": sb(32, "uint16"),
+    "zo": sb(8, "uint16"),
+    "nq": sb(32), "z32": sb(32),
+    "B": sb(128 * R),
+    "Q": sb(128 * R),
+    "bm": sb(128 * R), "cmp": sb(640 * R, BF), "junk": sb(640 * R, BF), "jj": sb(128 * R), "lr": sb(4 * R),
+    "ab": sb(128 * R), "wv": sb(128 * R), "wj": sb(128 * R, BF), "wvt": sb(128 * R), "wjt": sb(128 * R, BF), "vc": sb(R),
+    "jcol": sb(R), "bv": sb(32 * R), "vt": sb(32 * R), "gg": sb(96 * R), "c2": sb(96 * R), "n2": sb(R), "w2": sb(32 * R),
+    "w2x": sb(80 * R), "lf": sb(R), "lb": sb(32 * R), "lt": sb(32 * R), "ind": sb(32 * R), "indt": sb(32 * R), "tt": sb(R),
+    "pen": sb(4 * R), "sm": sb(4 * R), "mm": sb(4 * R), "m25": sb(4 * R), "sc": sb(4 * R), "sb": sb(128), "sr": sb(128),
+    "yo": sb(512), "ps": ("psum", [128, 2048], "float32"), "py": ("psum", [128, 2048], "float32"),
 }
 for _b in range(R):
-    SCRATCH["of%d" % _b] = ("sbuf", [128, 2], "uint16")
-    SCRATCH["mq%d" % _b] = ("sbuf", [128, 128], "float8_e4m3fn_x4")
-    SCRATCH["ms%d" % _b] = ("sbuf", [128, 128], "uint8")
+    SCRATCH["of%d" % _b] = sb(2, "uint16")
+    SCRATCH["mq%d" % _b] = sb(128, F8)
+    SCRATCH["ms%d" % _b] = sb(128, U8)
 
 SEMAPHORES = ["sv", "sa", "st", "sg", "du", "dw", "dse", "loc"]
 SEMAPHORES += ["dx%d" % i for i in range(4)]
-SEMAPHORES += ["%s%d" % (n, b) for n in ("near", "far", "dy", "dch") for b in range(R)]
+SEMAPHORES += ["%s%d" % (n, b) for n in ("nq", "nz", "far", "dy", "dch") for b in range(R)]
 
 
 def mask_of(engines):
@@ -92,12 +59,19 @@ def rank_program(g, core, T, topo):
     if rank is None:
         return
     cores = list(T.cores)
-    here = topo.chip(core)
-    mate_rank = [r for r in range(len(cores)) if r != rank and topo.chip(cores[r]) == here][0]
-    lo = min(rank, mate_rank)
-    peers = [r for r in range(len(cores)) if topo.chip(cores[r]) != here and r % 2 == rank % 2]
-    far_eng = topo.engines(core, cores[peers[0]])
-    near_eng = topo.engines(core, cores[mate_rank])[:len(far_eng)]
+    chips = []
+    for c in cores:
+        if topo.chip(c) not in chips:
+            chips.append(topo.chip(c))
+    on = lambda ch: [r for r in range(len(cores)) if topo.chip(cores[r]) == ch]
+    at = chips.index(topo.chip(core))
+    pair = on(chips[at])
+    mate = [r for r in pair if r != rank]
+    ahead = on(chips[(at + 1) % len(chips)])
+    rest = [on(chips[(at + k) % len(chips)])[pair.index(rank)] for k in (3, 2)]
+    far_eng = topo.engines(core, cores[ahead[0]])
+    near_eng = [e for e in topo.engines(core, cores[mate[0]]) if e not in far_eng]
+    n_far = len(far_eng) * 2 * (len(ahead) + len(rest))
 
     Q = {"v": g.vector, "a": g.scalar, "t": g.tensor, "g": g, "s": g.sync}
     count = {"v": 0, "a": 0, "t": 0, "g": 0}
@@ -155,38 +129,47 @@ def rank_program(g, core, T, topo):
         wait("t", deps)
         return done("t", g.tensor.matmul_mx(out, lq, ls, rq, rs, True, True))
 
-    def load(q, out, in_, sem, *deps, n=1):
+    def load(q, out, in_, sem, *deps):
         wait(q, deps)
         Q[q].dma_start(out, in_).then_inc(T.sem[sem], 16)
-        return (sem, 16 * n)
+        return (sem, 16)
 
-    lu = load("a", T.ut[:], T.u[:], "du")
+    def send(view, *groups):
+        g.remote_dma_fused([
+            RemoteDMATransfer(dst_ids=[DstId(rid=topo.addr(cores[r])[0], pnc=topo.addr(cores[r])[1]) for r in to],
+                              dma_engine_mask=mask_of(eng), remote_sem=T.sem[arr], srcs=[view], dsts=[view for r in to])
+            for to, eng, arr in groups], local_sem=T.sem.loc)
+
+    lu = load("a", T.ut[:, 0:64], T.u[:, 0:64], "du")
     lx = [load("s" if i % 2 == 0 else "a", T.xt[:, 512 * i:512 * i + 512], T.x[:, 512 * i:512 * i + 512], "dx%d" % i)
           for i in range(4)]
-    lw = load("s", T.wt[:], T.w[:], "dw")
+    lw = load("s", T.wt[:], T.w[:], "dw", lx[0])
 
     iota = lambda out, pat, cm, **kw: done("g", g.iota(out, pat, 0, cm, **kw))
     flag = {"allow_small_or_imprecise_dtypes": True}
     k_zo = fill(T.zo[:], 0)
+    k_u = fill(T.ut[:, 64:512], 0.0)
     k_ip = iota(T.ip[:], [[0, 1]], 1)
     k_ki = iota(T.ki[:], [[1, 32]], 0, **flag)
     k_16 = iota(T.k16[:], [[0, 2], [1, 16]], 0, **flag)
-    k_j4 = iota(T.j4[:], [[32, 4]], 4, **flag)
+    k_c4 = iota(T.c4[:], [[32, 4]], 0, **flag)
     k_pm = iota(T.pm[:], [[32, 4], [128, 4], [16, 2]], 0, **flag)
-    fill(T.nq[:], -0.25)
+    k_nq = fill(T.nq[:], -0.25)
     k_z = fill(T.z32[:], 0.0)
     k_gg = fill(T.gg[:], -BIG)
     a1 = ts(T.ir[:, 0:1], T.ip[:], 31, A.bitwise_and, k_ip)
     a2 = ts(T.ir[:, 1:2], T.ip[:], 15, A.bitwise_and)
+    a3 = vcopy(T.rc[:, 3:4], T.ip[:])
     k_rc = vcopy(T.rc[:, 0:2], T.ir[:], a1, a2)
-    k_r3 = ts(T.rc[:, 2:3], T.rc[:, 0:1], 3.0, A.mult, k_rc)
+    ts(T.rc[:, 2:3], T.rc[:, 3:4], T.rc[:, 0:1], A.subtract, k_rc, a3, s2=1.0 / 32, op1=A.mult)
     ts(T.kim[:], T.k16[:], T.rc[:, 0:1], A.subtract, k_16)
     k_mb = ts(T.mbig[:], T.ki[:], T.rc[:, 0:1], A.is_ge, k_ki, s2=BIG, op1=A.mult)
     ts(T.rb[:], T.z32[:], T.rc[:, 0:1], A.add, k_z)
     k_po = ts(T.po[:], T.pm[:], T.rc[:, 1:2], A.add, k_pm)
-    k_con = ts(T.jc[:], T.j4[:], T.rc[:, 2:3], A.subtract, k_j4, k_r3)
+    k_jn = ts(T.jn[:], T.c4[:], T.rc[:, 0:1], A.add, k_c4)
+    k_con = ts(T.nj[:], T.jn[:], -1.0, A.mult, k_jn)
 
-    qu = quant(T.uq[:], T.us[:], T.ut[:], lu)
+    qu = quant(T.uq[:], T.us[:], T.ut[:], lu, k_u)
     u1 = vcopy(T.vq[:].bitcast(dt.uint32), T.uq[:].bitcast(dt.uint32).indirect(T.zo[:, 0:8]), qu, k_zo)
     u2 = act(T.vs[:], T.us[:].indirect(T.zo[:, 0:8]), COPY, qu, k_zo)
     tq, qx = [], []
@@ -204,8 +187,7 @@ def rank_program(g, core, T, topo):
     tb = [turn(T.B[:, 0:128], T.Q[:, 0:128], *tq, k_con)] * 4
     bank_free = list(tq)
     y_todo = []
-    qw = perm = None
-    t_m = [None] * 4
+    qw = perm = sc = None
 
     def span(a, n):
         return slice(32 * a, 32 * a + 32 * n)
@@ -231,27 +213,26 @@ def rank_program(g, core, T, topo):
             d.append(tt(T.cmp[:, w + 128:w + 160], T.Q[:, o + 32 * c:o + 32 * c + 32],
                         T.bm[:, o + 32 * c:o + 32 * c + 32], A.is_equal, bm[c]))
             lr.append(act(T.junk[:, w:w + 160], T.cmp[:, w:w + 160], COPY, d, accum_out=T.lr[:, 4 * b + c:4 * b + c + 1]))
-
-        def onehot(dst, c, val):
-            return ts(dst[:, o + 32 * c:o + 32 * c + 32], T.ki[:], T.lr[:, 4 * b + c:4 * b + c + 1], A.is_equal, lr[c],
-                      s2=val, op1=A.mult)
-        wv = [onehot(T.wv, c, T.B[:, o + 32 * c:o + 32 * c + 1]) for c in range(4)]
-        wj = [onehot(T.wj, 0, T.jc[:, 0:1])]
+        cc = [slice(o + 32 * c, o + 32 * c + 32) for c in range(4)]
+        lc = [T.lr[:, 4 * b + c:4 * b + c + 1] for c in range(4)]
+        wv = [ts(T.wv[:, cc[c]], T.ki[:], lc[c], A.is_equal, lr[c], s2=T.B[:, o + 32 * c:o + 32 * c + 1], op1=A.mult)
+              for c in range(4)]
+        ab = [act(T.ab[:, cc[c]], T.ki[:], ABS, lr[c], k_ki, scale=-1.0, bias=lc[c]) for c in range(4)]
+        wj = [act(T.wj[:, cc[c]], T.ab[:, cc[c]], RELU, ab[c], k_con, scale=T.nj[:, c:c + 1], bias=T.jn[:, c:c + 1])
+              for c in range(4)]
         t2 = turn(T.wvt[:, o:o + 128], T.wv[:, o:o + 128], wv)
-        wj += [onehot(T.wj, c, T.jc[:, c:c + 1]) for c in (1, 2)]
         vc = red(T.vc[:, b:b + 1], T.wvt[:, o:o + 128], A.add, t2)
-        wj.append(onehot(T.wj, 3, T.jc[:, 3:4]))
         v32 = slice(32 * b, 32 * b + 32)
         bv = ts(T.bv[:, v32], T.z32[:], T.vc[:, b:b + 1], A.add, vc)
-        tj = turn(T.wjt[:, o:o + 128], T.wj[:, o:o + 128], wj)
         t3 = turn(T.vt[:, v32], T.bv[:, v32], bv)
+        tj = turn(T.wjt[:, o:o + 128], T.wj[:, o:o + 128], wj)
 
         cp = []
         for i, (to, fr, slot, half) in enumerate(moves):
-            at = 96 * b + 48 * half + 16 * slot
-            dst, src = T.gg[to, at:at + 16], T.vt[fr, 32 * b:32 * b + 16]
+            k = 96 * b + 48 * half + 16 * slot
+            dst, src = T.gg[to, k:k + 16], T.vt[fr, 32 * b:32 * b + 16]
             cp.append(vcopy(dst, src, t3, k_gg) if i % 2 == 0 else act(dst, src, COPY, t3, k_gg))
-        jcol = act(T.jj[:, o:o + 128], T.wjt[:, o:o + 128], COPY, tj, accum_out=T.jcol[:, b:b + 1])
+        jcol = act(T.jj[:, o:o + 128], T.wjt[:, o:o + 128], IDENT, tj, bias=T.rc[:, 2:3], accum_out=T.jcol[:, b:b + 1])
         g0 = 96 * b
         f1 = ts(T.c2[:, g0:g0 + 48], T.gg[:, g0:g0 + 48], T.vc[:, b:b + 1], A.is_ge, cp)
         f2 = ts(T.c2[:, g0 + 48:g0 + 96], T.gg[:, g0 + 48:g0 + 96], T.vc[:, b:b + 1], A.is_gt)
@@ -261,39 +242,34 @@ def rank_program(g, core, T, topo):
         t4 = turn(T.w2x[:, x0:x0 + 32], T.w2[:, v32], w2)
         cp = []
         for i, (to, fr, slot, half) in enumerate(moves):
-            at = x0 + 32 + 16 * slot
-            dst, src = T.w2x[to, at:at + 16], T.w2x[fr, x0:x0 + 16]
-            cp.append(vcopy(dst, src, t4) if i % 2 == 0 else act(dst, src, COPY, t4))
+            k = x0 + 32 + 16 * slot
+            dst, src = T.w2x[to, k:k + 16], T.w2x[fr, x0:x0 + 16]
+            cp.append(vcopy(dst, src, t4) if i % 2 == 0 or i == 9 else act(dst, src, COPY, t4))
         lf = red(T.lf[:, b:b + 1], T.w2x[:, x0:x0 + 80], A.add, cp, t4)
         of = T["of%d" % b]
         mq, ms = T["mq%d" % b], T["ms%d" % b]
         oo = vcopy(of[:, 0:1], T.lf[:, b:b + 1], lf)
         mine = slice(16 * rank, 16 * rank + 16)
-        both = slice(16 * lo, 16 * lo + 32)
+        both = slice(16 * pair[0], 16 * pair[0] + 32)
         pk = vcopy(mq[:, mine].bitcast(dt.uint32), T.xq[:].bitcast(dt.uint32).indirect(of[:, 0:1]), oo, qx)
         pz = act(ms[:, mine], T.xs[:].indirect(of[:, 0:1]), COPY, oo, qx)
 
-        near, far = "near%d" % b, "far%d" % b
-        rid, pid = topo.addr(cores[mate_rank])[:2]
+        far = "far%d" % b
+        arr_q, arr_z = ("nq%d" % b, len(near_eng)), ("nz%d" % b, len(near_eng))
         wait("g", [pk])
-        g.remote_dma(mq[:, mine].bitcast(dt.uint8), mq[:, mine].bitcast(dt.uint8), T.sem[near], T.sem.loc, pid, rid,
-                     mask_of(near_eng))
+        send(mq[:, mine].bitcast(dt.uint8), (mate, near_eng, arr_q[0]), (ahead, far_eng, far))
         wait("g", [pz])
-        g.remote_dma(ms[:, mine], ms[:, mine], T.sem[near], T.sem.loc, pid, rid, mask_of(near_eng))
-        arr1 = (near, 2 * len(near_eng))
-        wait("g", [arr1])
-        ids = [DstId(rid=topo.addr(cores[r])[0], pnc=topo.addr(cores[r])[1]) for r in peers]
-        for view in (mq[:, both].bitcast(dt.uint8), ms[:, both]):
-            g.remote_dma_fused([RemoteDMATransfer(dst_ids=ids, dma_engine_mask=mask_of(far_eng), remote_sem=T.sem[far],
-                                                  srcs=[view], dsts=[view for r in peers])], local_sem=T.sem.loc)
-        arr2 = (far, 2 * len(far_eng) * len(peers))
+        send(ms[:, mine], (mate, near_eng, arr_z[0]), (ahead, far_eng, far))
+        wait("g", [arr_q])
+        send(mq[:, both].bitcast(dt.uint8), (rest, far_eng, far))
+        wait("g", [arr_z])
+        send(ms[:, both], (rest, far_eng, far))
+        arrived = [arr_q, arr_z, (far, n_far)]
 
         if b == 0:
             p1 = vcopy(T.pq[:].bitcast(dt.uint32), T.xq[:].bitcast(dt.uint32).indirect(T.po[:]), k_po)
             p2 = act(T.pz[:], T.xs[:].indirect(T.po[:]), COPY, k_po, qx)
-            qw = quant(T.wq[:], T.ws[:], T.wt[:], lw)
             perm = [p1, p2]
-            sc = None
         if b < R - 1:
             i1 = ts(T.ind[:, v32], T.rb[:], T.n2[:, b:b + 1], A.add, s2=16.0, op1=A.is_lt)
             i2 = turn(T.indt[:, v32], T.ind[:, v32], i1)
@@ -301,9 +277,11 @@ def rank_program(g, core, T, topo):
             b4 = slice(4 * b, 4 * b + 4)
             i4 = ts(T.pen[:, b4], T.lr[:, b4], T.tt[:, b:b + 1], A.is_lt, i3, s2=-BIG, op1=A.mult)
             sm = tt(T.sm[:, b4], T.B[:, o:o + 128:32], T.pen[:, b4], A.add, i4)
+        if b == 0:
+            qw = quant(T.wq[:], T.ws[:], T.wt[:], lw)
         l1 = ts(T.lb[:, v32], T.z32[:], T.lf[:, b:b + 1], A.add)
         l2 = turn(T.lt[:, v32], T.lb[:, v32], l1)
-        och = load("s", T.ch[b:b + 1, :], T.lt[0:1, 32 * b:32 * b + 16], "dch%d" % b, l2)
+        load("s", T.ch[b:b + 1, :], T.lt[0:1, 32 * b:32 * b + 16], "dch%d" % b, l2)
         if b == 0:
             sc = vcopy(T.sc[:, 0:4], T.B[:, 0:128:32])
         else:
@@ -319,7 +297,7 @@ def rank_program(g, core, T, topo):
             f()
         y_todo = []
 
-        ready = [arr1, arr2, pk, pz]
+        ready = arrived + [pk, pz]
         if b < R - 1:
             tm = []
             for c in range(4):
@@ -327,16 +305,14 @@ def rank_program(g, core, T, topo):
                 tm.append(mm(T.ps[:, 512 * c:512 * c + 128], T.pq[:, k], T.pz[:, k], mq[:], ms[:], *ready, *perm, *bank_free))
             n = 128 * (b + 1)
             rd, tb = [None] * 4, [None] * 4
-
-            def fall(c):
-                i = 4 * b + c
-                tb[c] = ts(T.B[:, n + 32 * c:n + 32 * c + 32], T.nq[:], T.mm[:, i:i + 1], A.mult, rd[c], sm,
-                           s2=T.sm[:, i:i + 1], op1=A.add)
             for c in range(4):
-                rd[c] = red(T.mm[:, 4 * b + c:4 * b + c + 1], T.ps[:, 512 * c:512 * c + 128], A.max, tm[c])
-                if c > 0:
-                    fall(c - 1)
-            fall(3)
+                i = 4 * b + c
+                rd[c] = red(T.mm[:, i:i + 1], T.ps[:, 512 * c:512 * c + 128], A.max, tm[c])
+                out, m1, s1 = T.B[:, n + 32 * c:n + 32 * c + 32], T.mm[:, i:i + 1], T.sm[:, i:i + 1]
+                if c < 3:
+                    tb[c] = act(out, T.nq[:], IDENT, rd[c], sm, k_nq, scale=m1, bias=s1)
+                else:
+                    tb[c] = ts(out, T.nq[:], m1, A.mult, rd[c], sm, s2=s1, op1=A.add)
             bank_free = list(rd)
         ty = mm(T.py[:, 512 * b:512 * b + 128], T.wq[:], T.ws[:], mq[:], ms[:], *ready, qw)
 
@@ -348,8 +324,6 @@ def rank_program(g, core, T, topo):
     for f in y_todo:
         f()
 
-    sent = R * 2 * (len(near_eng) + len(far_eng))
-    last = [("loc", sent), ("dse", 64)] + [("s" + q, count[q]) for q in count]
+    last = [("loc", R * (2 * len(near_eng) + 4 * len(far_eng))), ("dse", 64)] + [("s" + q, count[q]) for q in count]
     last += [("dy%d" % b, 16) for b in range(R)] + [("dch%d" % b, 16) for b in range(R)]
-    last += [("far%d" % b, 2 * len(far_eng) * len(peers)) for b in range(R)]
     wait("g", last)

from concourse.bass import DstId, RemoteDMATransfer
from concourse.mybir import dt, AluOpType, AxisListType, ActivationFunctionType

R = 4
COPY = ActivationFunctionType.Copy
IDENT = ActivationFunctionType.Identity
ABS = ActivationFunctionType.Abs
RELU = ActivationFunctionType.Relu
A = AluOpType
BIG = 1e29


def sb(n, d="float32"):
    return ("sbuf", [128, n], d)


F8, U8, BF = "float8_e4m3fn_x4", "uint8", "bfloat16"
SCRATCH = {
    "xt": sb(2048, BF), "ut": sb(512, BF), "wt": sb(512, BF),
    "xq": sb(512, F8), "xs": sb(512, U8),
    "pq": sb(512, F8), "pz": sb(512, U8),
    "uq": sb(128, F8), "us": sb(128, U8), "vq": sb(128, F8), "vs": sb(128, U8), "wq": sb(128, F8), "ws": sb(128, U8),
    "ip": sb(1, "int32"), "ir": sb(2, "int32"),
    "rc": sb(4),
    "ki": sb(32),
    "k16": sb(32),
    "kim": sb(32),
    "mbig": sb(32),
    "rb": sb(32),
    "c4": sb(4), "jn": sb(4), "nj": sb(4),
    "pm": sb(32), "po": sb(32, "uint16"),
    "zo": sb(8, "uint16"),
    "nq": sb(32), "z32": sb(32),
    "B": sb(128 * R),
    "Q": sb(128 * R),
    "bm": sb(128 * R), "cmp": sb(640 * R, BF), "junk": sb(640 * R, BF), "jj": sb(128 * R), "lr": sb(4 * R),
    "ab": sb(128 * R), "wv": sb(128 * R), "wj": sb(128 * R, BF), "wvt": sb(128 * R), "wjt": sb(128 * R, BF), "vc": sb(R),
    "jcol": sb(R), "bv": sb(32 * R), "vt": sb(32 * R), "gg": sb(96 * R), "c2": sb(96 * R), "n2": sb(R), "w2": sb(32 * R),
    "w2x": sb(80 * R), "lf": sb(R), "lb": sb(32 * R), "lt": sb(32 * R), "ind": sb(32 * R), "indt": sb(32 * R), "tt": sb(R),
    "pen": sb(4 * R), "sm": sb(4 * R), "mm": sb(4 * R), "m25": sb(4 * R), "sc": sb(4 * R), "sb": sb(128), "sr": sb(128),
    "yo": sb(512), "ps": ("psum", [128, 2048], "float32"), "py": ("psum", [128, 2048], "float32"),
}
for _b in range(R):
    SCRATCH["of%d" % _b] = sb(2, "uint16")
    SCRATCH["mq%d" % _b] = sb(128, F8)
    SCRATCH["ms%d" % _b] = sb(128, U8)

SEMAPHORES = ["sv", "sa", "st", "sg", "du", "dw", "dse", "loc"]
SEMAPHORES += ["dx%d" % i for i in range(4)]
SEMAPHORES += ["%s%d" % (n, b) for n in ("nq", "nz", "far", "dy", "dch") for b in range(R)]


def mask_of(engines):
    return sum(1 << e for e in engines)


def rank_program(g, core, T, topo):
    rank = T.rank_of(core)
    if rank is None:
        return
    cores = list(T.cores)
    chips = []
    for c in cores:
        if topo.chip(c) not in chips:
            chips.append(topo.chip(c))
    on = lambda ch: [r for r in range(len(cores)) if topo.chip(cores[r]) == ch]
    at = chips.index(topo.chip(core))
    pair = on(chips[at])
    mate = [r for r in pair if r != rank]
    ahead = on(chips[(at + 1) % len(chips)])
    rest = [on(chips[(at + k) % len(chips)])[pair.index(rank)] for k in (3, 2)]
    far_eng = topo.engines(core, cores[ahead[0]])
    near_eng = [e for e in topo.engines(core, cores[mate[0]]) if e not in far_eng]
    n_far = len(far_eng) * 2 * (len(ahead) + len(rest))

    Q = {"v": g.vector, "a": g.scalar, "t": g.tensor, "g": g, "s": g.sync}
    count = {"v": 0, "a": 0, "t": 0, "g": 0}
    seen = {k: {} for k in Q}

    def wait(q, deps):
        need = {}
        for d in deps:
            for s, n in (d if isinstance(d, list) else [d]):
                need[s] = max(need.get(s, 0), n)
        for s, n in need.items():
            if seen[q].get(s, 0) < n:
                Q[q].wait_ge(T.sem[s], n)
                seen[q][s] = n

    def done(q, ins):
        count[q] += 1
        ins.then_inc(T.sem["s" + q], 1)
        return ("s" + q, count[q])

    def ts(out, in0, s1, op0, *deps, s2=None, op1=None):
        wait("v", deps)
        if op1 is None:
            return done("v", g.vector.tensor_scalar(out, in0, s1, None, op0))
        return done("v", g.vector.tensor_scalar(out, in0, s1, s2, op0, op1))

    def tt(out, a, b, op, *deps):
        wait("v", deps)
        return done("v", g.vector.tensor_tensor(out, a, b, op))

    def red(out, in_, op, *deps):
        wait("v", deps)
        return done("v", g.vector.tensor_reduce(out, in_, AxisListType.X, op))

    def turn(out, in_, *deps):
        wait("v", deps)
        return done("v", g.vector.transpose(out, in_))

    def vcopy(out, in_, *deps):
        wait("v", deps)
        return done("v", g.vector.tensor_copy(out, in_))

    def fill(out, c):
        return done("v", g.vector.memset(out, c))

    def quant(q, s, x, *deps):
        wait("v", deps)
        return done("v", g.vector.quantize_mx(q, s, x))

    def act(out, in_, func, *deps, **kw):
        wait("a", deps)
        return done("a", g.scalar.activation(out, in_, func, **kw))

    def mm(out, lq, ls, rq, rs, *deps):
        wait("t", deps)
        return done("t", g.tensor.matmul_mx(out, lq, ls, rq, rs, True, True))

    def load(q, out, in_, sem, *deps):
        wait(q, deps)
        Q[q].dma_start(out, in_).then_inc(T.sem[sem], 16)
        return (sem, 16)

    def send(view, *groups):
        g.remote_dma_fused([
            RemoteDMATransfer(dst_ids=[DstId(rid=topo.addr(cores[r])[0], pnc=topo.addr(cores[r])[1]) for r in to],
                              dma_engine_mask=mask_of(eng), remote_sem=T.sem[arr], srcs=[view], dsts=[view for r in to])
            for to, eng, arr in groups], local_sem=T.sem.loc)

    lu = load("a", T.ut[:, 0:64], T.u[:, 0:64], "du")
    lx = [load("s" if i % 2 == 0 else "a", T.xt[:, 512 * i:512 * i + 512], T.x[:, 512 * i:512 * i + 512], "dx%d" % i)
          for i in range(4)]
    lw = load("s", T.wt[:], T.w[:], "dw", lx[0])

    iota = lambda out, pat, cm, **kw: done("g", g.iota(out, pat, 0, cm, **kw))
    flag = {"allow_small_or_imprecise_dtypes": True}
    k_zo = fill(T.zo[:], 0)
    k_u = fill(T.ut[:, 64:512], 0.0)
    k_ip = iota(T.ip[:], [[0, 1]], 1)
    k_ki = iota(T.ki[:], [[1, 32]], 0, **flag)
    k_16 = iota(T.k16[:], [[0, 2], [1, 16]], 0, **flag)
    k_c4 = iota(T.c4[:], [[32, 4]], 0, **flag)
    k_pm = iota(T.pm[:], [[32, 4], [128, 4], [16, 2]], 0, **flag)
    k_nq = fill(T.nq[:], -0.25)
    k_z = fill(T.z32[:], 0.0)
    k_gg = fill(T.gg[:], -BIG)
    a1 = ts(T.ir[:, 0:1], T.ip[:], 31, A.bitwise_and, k_ip)
    a2 = ts(T.ir[:, 1:2], T.ip[:], 15, A.bitwise_and)
    a3 = vcopy(T.rc[:, 3:4], T.ip[:])
    k_rc = vcopy(T.rc[:, 0:2], T.ir[:], a1, a2)
    ts(T.rc[:, 2:3], T.rc[:, 3:4], T.rc[:, 0:1], A.subtract, k_rc, a3, s2=1.0 / 32, op1=A.mult)
    ts(T.kim[:], T.k16[:], T.rc[:, 0:1], A.subtract, k_16)
    k_mb = ts(T.mbig[:], T.ki[:], T.rc[:, 0:1], A.is_ge, k_ki, s2=BIG, op1=A.mult)
    ts(T.rb[:], T.z32[:], T.rc[:, 0:1], A.add, k_z)
    k_po = ts(T.po[:], T.pm[:], T.rc[:, 1:2], A.add, k_pm)
    k_jn = ts(T.jn[:], T.c4[:], T.rc[:, 0:1], A.add, k_c4)
    k_con = ts(T.nj[:], T.jn[:], -1.0, A.mult, k_jn)

    qu = quant(T.uq[:], T.us[:], T.ut[:], lu, k_u)
    u1 = vcopy(T.vq[:].bitcast(dt.uint32), T.uq[:].bitcast(dt.uint32).indirect(T.zo[:, 0:8]), qu, k_zo)
    u2 = act(T.vs[:], T.us[:].indirect(T.zo[:, 0:8]), COPY, qu, k_zo)
    tq, qx = [], []
    for i in range(4):
        c = slice(128 * i, 128 * i + 128)
        qx.append(quant(T.xq[:, c], T.xs[:, c], T.xt[:, 512 * i:512 * i + 512], lx[i]))
    for i in range(4):
        c = slice(128 * i, 128 * i + 128)
        h = slice(32 * i, 32 * i + 32)
        t = mm(T.ps[:, 512 * i:512 * i + 128], T.vq[:], T.vs[:], T.xq[:, c], T.xs[:, c], u1, u2, qx[i])
        if i % 2 == 0:
            tq.append(vcopy(T.Q[h, 0:128], T.ps[h, 512 * i:512 * i + 128], t))
        else:
            tq.append(act(T.Q[h, 0:128], T.ps[h, 512 * i:512 * i + 128], COPY, t))
    tb = [turn(T.B[:, 0:128], T.Q[:, 0:128], *tq, k_con)] * 4
    bank_free = list(tq)
    y_todo = []
    qw = perm = sc = None

    def span(a, n):
        return slice(32 * a, 32 * a + 32 * n)
    moves = [(span(0, 2), span(2, 2), 0, 1), (span(2, 2), span(0, 2), 0, 0)]
    for x, slot in ((1, 1), (3, 2)):
        for a in range(4):
            moves.append((span(a, 1), span(a ^ x, 1), slot, 1 if (a ^ x) > a else 0))

    for b in range(R):
        o = 128 * b
        if b > 0:
            tq = [turn(T.Q[:, o:o + 128], T.B[:, o:o + 128], *tb)]
        bm = [act(T.bm[:, o + 32 * c:o + 32 * c + 32], T.mbig[:], IDENT, tb[c], k_mb,
                  bias=T.B[:, o + 32 * c:o + 32 * c + 1]) for c in range(4)]
        lr = []
        for c in range(4):
            s = T.B[:, o + 32 * c:o + 32 * c + 1]
            w = 640 * b + 160 * c
            d = []
            if c > 0:
                d.append(ts(T.cmp[:, w:w + 32 * c], T.Q[:, o:o + 32 * c], s, A.is_ge, tq, tb))
            d.append(ts(T.cmp[:, w + 32 * c:w + 128], T.Q[:, o + 32 * c:o + 128], s, A.is_gt, tq, tb))
            d.append(tt(T.cmp[:, w + 128:w + 160], T.Q[:, o + 32 * c:o + 32 * c + 32],
                        T.bm[:, o + 32 * c:o + 32 * c + 32], A.is_equal, bm[c]))
            lr.append(act(T.junk[:, w:w + 160], T.cmp[:, w:w + 160], COPY, d, accum_out=T.lr[:, 4 * b + c:4 * b + c + 1]))
        cc = [slice(o + 32 * c, o + 32 * c + 32) for c in range(4)]
        lc = [T.lr[:, 4 * b + c:4 * b + c + 1] for c in range(4)]
        wv = [ts(T.wv[:, cc[c]], T.ki[:], lc[c], A.is_equal, lr[c], s2=T.B[:, o + 32 * c:o + 32 * c + 1], op1=A.mult)
              for c in range(4)]
        ab = [act(T.ab[:, cc[c]], T.ki[:], ABS, lr[c], k_ki, scale=-1.0, bias=lc[c]) for c in range(4)]
        wj = [act(T.wj[:, cc[c]], T.ab[:, cc[c]], RELU, ab[c], k_con, scale=T.nj[:, c:c + 1], bias=T.jn[:, c:c + 1])
              for c in range(4)]
        t2 = turn(T.wvt[:, o:o + 128], T.wv[:, o:o + 128], wv)
        vc = red(T.vc[:, b:b + 1], T.wvt[:, o:o + 128], A.add, t2)
        v32 = slice(32 * b, 32 * b + 32)
        bv = ts(T.bv[:, v32], T.z32[:], T.vc[:, b:b + 1], A.add, vc)
        t3 = turn(T.vt[:, v32], T.bv[:, v32], bv)
        tj = turn(T.wjt[:, o:o + 128], T.wj[:, o:o + 128], wj)

        cp = []
        for i, (to, fr, slot, half) in enumerate(moves):
            k = 96 * b + 48 * half + 16 * slot
            dst, src = T.gg[to, k:k + 16], T.vt[fr, 32 * b:32 * b + 16]
            cp.append(vcopy(dst, src, t3, k_gg) if i % 2 == 0 else act(dst, src, COPY, t3, k_gg))
        jcol = act(T.jj[:, o:o + 128], T.wjt[:, o:o + 128], IDENT, tj, bias=T.rc[:, 2:3], accum_out=T.jcol[:, b:b + 1])
        g0 = 96 * b
        f1 = ts(T.c2[:, g0:g0 + 48], T.gg[:, g0:g0 + 48], T.vc[:, b:b + 1], A.is_ge, cp)
        f2 = ts(T.c2[:, g0 + 48:g0 + 96], T.gg[:, g0 + 48:g0 + 96], T.vc[:, b:b + 1], A.is_gt)
        n2 = red(T.n2[:, b:b + 1], T.c2[:, g0:g0 + 96], A.add, f1, f2)
        w2 = ts(T.w2[:, v32], T.kim[:], T.n2[:, b:b + 1], A.is_equal, n2, jcol, s2=T.jcol[:, b:b + 1], op1=A.mult)
        x0 = 80 * b
        t4 = turn(T.w2x[:, x0:x0 + 32], T.w2[:, v32], w2)
        cp = []
        for i, (to, fr, slot, half) in enumerate(moves):
            k = x0 + 32 + 16 * slot
            dst, src = T.w2x[to, k:k + 16], T.w2x[fr, x0:x0 + 16]
            cp.append(vcopy(dst, src, t4) if i % 2 == 0 or i == 9 else act(dst, src, COPY, t4))
        lf = red(T.lf[:, b:b + 1], T.w2x[:, x0:x0 + 80], A.add, cp, t4)
        of = T["of%d" % b]
        mq, ms = T["mq%d" % b], T["ms%d" % b]
        oo = vcopy(of[:, 0:1], T.lf[:, b:b + 1], lf)
        mine = slice(16 * rank, 16 * rank + 16)
        both = slice(16 * pair[0], 16 * pair[0] + 32)
        pk = vcopy(mq[:, mine].bitcast(dt.uint32), T.xq[:].bitcast(dt.uint32).indirect(of[:, 0:1]), oo, qx)
        pz = act(ms[:, mine], T.xs[:].indirect(of[:, 0:1]), COPY, oo, qx)

        far = "far%d" % b
        arr_q, arr_z = ("nq%d" % b, len(near_eng)), ("nz%d" % b, len(near_eng))
        wait("g", [pk])
        send(mq[:, mine].bitcast(dt.uint8), (mate, near_eng, arr_q[0]), (ahead, far_eng, far))
        wait("g", [pz])
        send(ms[:, mine], (mate, near_eng, arr_z[0]), (ahead, far_eng, far))
        wait("g", [arr_q])
        send(mq[:, both].bitcast(dt.uint8), (rest, far_eng, far))
        wait("g", [arr_z])
        send(ms[:, both], (rest, far_eng, far))
        arrived = [arr_q, arr_z, (far, n_far)]

        if b == 0:
            p1 = vcopy(T.pq[:].bitcast(dt.uint32), T.xq[:].bitcast(dt.uint32).indirect(T.po[:]), k_po)
            p2 = act(T.pz[:], T.xs[:].indirect(T.po[:]), COPY, k_po, qx)
            perm = [p1, p2]
        if b < R - 1:
            i1 = ts(T.ind[:, v32], T.rb[:], T.n2[:, b:b + 1], A.add, s2=16.0, op1=A.is_lt)
            i2 = turn(T.indt[:, v32], T.ind[:, v32], i1)
            i3 = red(T.tt[:, b:b + 1], T.indt[:, v32], A.add, i2)
            b4 = slice(4 * b, 4 * b + 4)
            i4 = ts(T.pen[:, b4], T.lr[:, b4], T.tt[:, b:b + 1], A.is_lt, i3, s2=-BIG, op1=A.mult)
            sm = tt(T.sm[:, b4], T.B[:, o:o + 128:32], T.pen[:, b4], A.add, i4)
        if b == 0:
            qw = quant(T.wq[:], T.ws[:], T.wt[:], lw)
        l1 = ts(T.lb[:, v32], T.z32[:], T.lf[:, b:b + 1], A.add)
        l2 = turn(T.lt[:, v32], T.lb[:, v32], l1)
        load("s", T.ch[b:b + 1, :], T.lt[0:1, 32 * b:32 * b + 16], "dch%d" % b, l2)
        if b == 0:
            sc = vcopy(T.sc[:, 0:4], T.B[:, 0:128:32])
        else:
            p4, b4 = slice(4 * b - 4, 4 * b), slice(4 * b, 4 * b + 4)
            m1 = ts(T.m25[:, p4], T.mm[:, p4], -0.25, A.mult)
            sc = tt(T.sc[:, b4], T.sc[:, p4], T.m25[:, p4], A.add, m1, sc)
        if b == R - 1:
            e = [ts(T.sb[:, 32 * c:32 * c + 32], T.z32[:], T.sc[:, 4 * b + c:4 * b + c + 1], A.add, sc) for c in range(4)]
            e = turn(T.sr[:], T.sb[:], e)
            for a in range(4):
                load("s", T.se[0:1, 128 * a:128 * a + 128], T.sr[32 * a:32 * a + 1, :], "dse", e)
        for f in y_todo:
            f()
        y_todo = []

        ready = arrived + [pk, pz]
        if b < R - 1:
            tm = []
            for c in range(4):
                k = slice(128 * c, 128 * c + 128)
                tm.append(mm(T.ps[:, 512 * c:512 * c + 128], T.pq[:, k], T.pz[:, k], mq[:], ms[:], *ready, *perm, *bank_free))
            n = 128 * (b + 1)
            rd, tb = [None] * 4, [None] * 4
            for c in range(4):
                i = 4 * b + c
                rd[c] = red(T.mm[:, i:i + 1], T.ps[:, 512 * c:512 * c + 128], A.max, tm[c])
                out, m1, s1 = T.B[:, n + 32 * c:n + 32 * c + 32], T.mm[:, i:i + 1], T.sm[:, i:i + 1]
                if c < 3:
                    tb[c] = act(out, T.nq[:], IDENT, rd[c], sm, k_nq, scale=m1, bias=s1)
                else:
                    tb[c] = ts(out, T.nq[:], m1, A.mult, rd[c], sm, s2=s1, op1=A.add)
            bank_free = list(rd)
        ty = mm(T.py[:, 512 * b:512 * b + 128], T.wq[:], T.ws[:], mq[:], ms[:], *ready, qw)

        def put(b=b, ty=ty):
            k = slice(128 * b, 128 * b + 128)
            t = act(T.yo[:, k], T.py[:, 512 * b:512 * b + 128], COPY, ty)
            load("s", T.y[:, k], T.yo[:, k], "dy%d" % b, t)
        y_todo.append(put)
    for f in y_todo:
        f()

    last = [("loc", R * (2 * len(near_eng) + 4 * len(far_eng))), ("dse", 64)] + [("s" + q, count[q]) for q in count]
    last += [("dy%d" % b, 16) for b in range(R)] + [("dch%d" % b, 16) for b in range(R)]
    wait("g", last)
